import numpy as np
import ml_dtypes


def mxq(x, axis, fmt="e4m3"):
    dtype, down = {"e4m3": (ml_dtypes.float8_e4m3fn, 7), "e5m2": (ml_dtypes.float8_e5m2, 14)}[fmt]
    v = np.moveaxis(np.asarray(x, np.float32).astype(ml_dtypes.bfloat16).astype(np.float64), axis, -1)
    blocks = v.reshape(v.shape[:-1] + (-1, 32))
    amax = np.abs(blocks).max(-1, keepdims=True)
    byte = np.maximum(np.where(amax > 0, np.frexp(amax)[1] - 1 + 127, 0) - down, 1)
    scale = np.exp2(byte - 127.0)
    codes = (blocks / scale).astype(np.float32).astype(dtype).astype(np.float64)
    return np.moveaxis((codes * scale).reshape(v.shape), -1, axis)


WIDE = False


def mx_kscale(k):
    if not WIDE:
        return np.ones(k)
    levels = np.array([10, -10, 5, -5, 0])
    if k % 512:
        return np.exp2(np.random.permutation(np.resize(levels, k // 32))).repeat(32)
    a = np.empty((k // 512, 16))
    for p in range(k // 512):
        a[p, :8] = np.random.permutation(np.resize(levels, 8))
        for g in range(8):
            far = levels[np.abs(levels - a[p, g]) >= 10]
            a[p, g + 8] = far[np.random.randint(len(far))]
    return np.exp2(a.ravel()).repeat(32)


def f64(x):
    return np.asarray(x).astype(np.float64)


def striped(idx):
    return np.tile(np.asarray(idx).reshape(-1, 16).T, (8, 1)).astype(np.uint16)


def unstriped(offs):
    return offs[:16].T.reshape(-1).astype(np.int64)


E2M1 = np.array([0.0, 0.5, 1.0, 1.5, 2.0, 3.0, 4.0, 6.0, -0.0, -0.5, -1.0, -1.5, -2.0, -3.0, -4.0, -6.0])


def pack_weight(w, fmt):
    k, n = w.shape
    w = f64(np.asarray(w, np.float32).astype(ml_dtypes.bfloat16)).reshape(k // 32, 32, n)
    amax = np.abs(w).max(1)
    if fmt == "e4m3":
        byte = np.frexp(amax)[1] - 1 + 127 - 7
    else:
        mant, ex = np.frexp(amax / 6.0)
        byte = np.where(mant > 0.5, ex, ex - 1) + 127
    byte = np.clip(np.where(amax > 0, byte, 1), 1, 254)
    scaled = (w * np.exp2(127.0 - byte)[:, None, :]).reshape(k, n).astype(np.float32)
    by_word = np.ascontiguousarray(scaled.reshape(k // 512, 128, 4, n).transpose(0, 1, 3, 2))
    if fmt == "e4m3":
        words = by_word.astype(ml_dtypes.float8_e4m3fn).view(np.uint8)
    else:
        c = by_word.astype(ml_dtypes.float4_e2m1fn).view(np.uint8) & 0xF
        words = (c[..., 0::2] | (c[..., 1::2] << 4)).reshape(k // 512, 128, 2 * n)
    return np.ascontiguousarray(words), np.ascontiguousarray(byte.astype(np.uint8).reshape(k // 512, 16, n))


def unpack_weight(words, scales, fmt):
    g, _, n = scales.shape
    words = np.ascontiguousarray(words).reshape(g, 128, n, -1)
    if fmt == "e4m3":
        vals = words.view(ml_dtypes.float8_e4m3fn).astype(np.float64)
    else:
        nib = np.empty((g, 128, n, 4), np.uint8)
        nib[..., 0::2] = words & 0xF
        nib[..., 1::2] = words >> 4
        vals = E2M1[nib]
    vals = vals * np.repeat(np.exp2(scales.astype(np.float64) - 127.0), 8, axis=1)[..., None]
    return vals.transpose(0, 1, 3, 2).reshape(g * 512, n)


def softplus(v):
    return np.log(1.0 + np.exp(v))


def sigmoid(v):
    return 1.0 / (1.0 + np.exp(-v))


D, T, U, I, J, G = 512, 1024, 1024, 256, 512, 64


def setup_inputs():
    n = np.random.standard_normal
    idx = np.random.permutation(T)[:I]
    idx2 = np.random.permutation(U)[:J]
    fd = mx_kscale(D)
    tabbp = pack_weight(n((D, U)) / fd[:, None], "e4m3")
    return {
        "taba": (n((D, T)) * 1 / np.sqrt(D) * fd[:, None]).astype(np.float32),
        "tabb_words": tabbp[0],
        "tabb_scales": tabbp[1],
        "reserve": (np.random.uniform(20.0, 100.0, (I, 1))).astype(np.float32),
        "stake": (n((I, G)) * 1.5).astype(np.float32),
        "old": (0.3 * n((I, J))).astype(np.float32),
        "offs": striped(idx),
        "offs2": striped(idx2),
    }


def reference(taba, tabb_words, tabb_scales, reserve, stake, old, offs, offs2):
    idx = unstriped(offs)
    idx2 = unstriped(offs2)
    tabbu = unpack_weight(tabb_words, tabb_scales, "e4m3")
    tabaidxq = mxq(f64(taba)[:, idx], 0, "e4m3")
    tabbidx2g = tabbu[:, idx2]
    s = tabaidxq.T @ tabbidx2g
    p = softplus(s)
    z = np.sum(p, axis=1, keepdims=True) + f64(reserve)
    s1g = p.reshape(I, G, J // G).sum(axis=2) / z
    ds1g = f64(stake) / (s1g * 64.0 + 1.0) * 64.0
    e1 = ds1g / z
    r1 = np.repeat(e1, J // G, axis=1)
    dz = np.sum(ds1g * p.reshape(I, G, J // G).sum(axis=2) / np.square(z) * (-1.0), axis=1, keepdims=True)
    dp = r1 + dz
    ds = dp * sigmoid(s)
    y = ds * 8.0 + f64(old)
    return y

@@ -1,0 +1,239 @@
+import math
+from contextlib import ExitStack
+
+import concourse.mybir as mybir
+
+D, T, U, I, J, G = 512, 1024, 1024, 256, 512, 64
+FLOPS = 2 * I * J * D
+
+F32 = mybir.dt.float32
+BF16 = mybir.dt.bfloat16
+I32 = mybir.dt.int32
+U32 = mybir.dt.uint32
+U16 = mybir.dt.uint16
+U8 = mybir.dt.uint8
+FP8X4 = mybir.dt.float8_e4m3fn_x4
+ALU = mybir.AluOpType
+ACT = mybir.ActivationFunctionType
+AX = mybir.AxisListType
+
+P = 128
+PACK = 4
+TILES = I // P
+GROUP = J // G
+HALF = GROUP // 2
+CAP = 10.875
+
+
+def tile_attend_bpairquota_kernel(tc, taba, tabb_words, tabb_scales, reserve, stake, old, offs, offs2, out):
+    nc = tc.nc
+    with ExitStack() as ctx:
+        sb = ctx.enter_context(tc.tile_pool(name="sb", bufs=1))
+        ps = ctx.enter_context(tc.psum_pool(name="ps", bufs=1))
+
+        list_a = sb.tile([P, I // 16], U16, name="list_a")
+        list_b = sb.tile([P, J // 16], U16, name="list_b")
+        b_words_all = sb.tile([P, U], U32, name="b_words_all", align_bytes=64)
+        b_scales_all = sb.tile([P, U], U8, name="b_scales_all", align_bytes=64)
+        planes = [sb.tile([P, T], F32, name="plane%d" % r, align_bytes=64) for r in range(PACK)]
+        reserve_sb = sb.tile([P, TILES], F32, name="reserve_sb")
+        stake_sb = sb.tile([P, TILES, G], F32, name="stake_sb")
+        old_sb = [sb.tile([P, J], F32, name="old%d" % t) for t in range(TILES)]
+
+        nc.vector.memset(b_scales_all[:].bitcast(I32), 0)
+        neg_cap = sb.tile([P, 1], F32, name="neg_cap")
+        nc.vector.memset(neg_cap[:], -CAP)
+
+        nc.sync.dma_start(list_b[:], offs2)
+        for q in range(4):
+            nc.scalar.dma_start(
+                b_scales_all[32 * q : 32 * q + 4, :].bitcast(I32),
+                tabb_scales[0, 4 * q : 4 * q + 4, :].bitcast(I32),
+            )
+        nc.sync.dma_start(
+            b_words_all[:].bitcast(I32),
+            tabb_words[0].rearrange("p n r -> p (n r)").bitcast(I32),
+        )
+        nc.sync.dma_start(list_a[:], offs)
+        taba_planes = taba.rearrange("(p r) t -> p r t", r=PACK)
+        for r in range(PACK):
+            nc.sync.dma_start(planes[r][:], taba_planes[:, r, :])
+        nc.sync.dma_start(stake_sb[:], stake.rearrange("(t p) g -> p t g", p=P))
+        with nc.allow_non_contiguous_dma(reason="one reserve value for each row"):
+            nc.sync.dma_start(reserve_sb[:], reserve.rearrange("(t p) o -> p (t o)", p=P))
+        for t in range(TILES):
+            nc.sync.dma_start(old_sb[t][:], old[t * P : (t + 1) * P, :])
+
+        floor = sb.tile([P, 1], F32, name="floor")
+        nc.scalar.activation(floor[:], neg_cap[:], ACT.Sigmoid)
+
+        b_scales = sb.tile([P, J], U8, name="b_scales", align_bytes=64)
+        b_words = sb.tile([P, J], U32, name="b_words", align_bytes=64)
+        b_scales_listed = sb.tile([P, J], U8, name="b_scales_listed", align_bytes=64)
+        nc.vector.tensor_copy(b_scales_listed[:], b_scales_all[:].indirect(list_b[:]))
+        nc.vector.tensor_copy(
+            b_words[:].rearrange("p (h g k) -> p g h k", h=2, k=HALF), b_words_all[:].indirect(list_b[:])
+        )
+        nc.vector.tensor_copy(
+            b_scales[:].bitcast(I32).rearrange("p (h g) -> p h g", h=2),
+            b_scales_listed[:].bitcast(I32).rearrange("p (g h) -> p h g", h=2),
+        )
+
+        woven = [sb.tile([P, P, PACK], BF16, name="woven%d" % t, align_bytes=64) for t in range(TILES)]
+        a_words = [sb.tile([P, P], U32, name="a_words%d" % t, align_bytes=64) for t in range(TILES)]
+        a_scales = [sb.tile([P, P], U8, name="a_scales%d" % t, align_bytes=64) for t in range(TILES)]
+        scores = [[ps.tile([P, G, HALF], F32, name="scores%d_%d" % (t, h)) for h in range(2)] for t in range(TILES)]
+        cols = P // 16
+
+        def gather(r, t):
+            nc.vector.tensor_copy(woven[t][:, :, r], planes[r][:].indirect(list_a[:, t * cols : (t + 1) * cols]))
+
+        for r in range(PACK - 1):
+            for t in range(TILES):
+                gather(r, t)
+        for t in range(TILES):
+            gather(PACK - 1, t)
+            nc.vector.quantize_mx(
+                out=a_words[t][:].bitcast(FP8X4),
+                scales=a_scales[t][:],
+                in_=woven[t][:].rearrange("p i r -> p (i r)"),
+            )
+            for h in range(2):
+                nc.tensor.matmul_mx(
+                    out=scores[t][h][:].rearrange("p g k -> p (g k)"),
+                    lhsT=a_words[t][:].bitcast(FP8X4),
+                    lhsT_scale=a_scales[t][:],
+                    rhs=b_words[:, h * (J // 2) : (h + 1) * (J // 2)].bitcast(FP8X4),
+                    rhs_scale=b_scales[:, h * (J // 2) : (h + 1) * (J // 2)],
+                    start=True,
+                    stop=True,
+                )
+
+        stake_sum = sb.tile([P, TILES], F32, name="stake_sum")
+        stake8 = sb.tile([P, TILES, G], F32, name="stake8")
+        for t in range(TILES):
+            nc.scalar.activation(
+                stake8[:, t], stake_sb[:, t], ACT.Copy, scale=1.0 / 8.0, accum_out=stake_sum[:, t : t + 1]
+            )
+        reserve64 = sb.tile([P, TILES], F32, name="reserve64")
+        nc.scalar.activation(reserve64[:], reserve_sb[:], ACT.Copy, scale=1.0 / 64.0)
+
+        miss = [sb.tile([P, 2, G, HALF], F32, name="miss%d" % t) for t in range(TILES)]
+        x = [sb.tile([P, G, HALF], F32, name="x%d" % t) for t in range(TILES)]
+        for t in range(TILES):
+            for h in range(2):
+                nc.scalar.activation(miss[t][:, h], scores[t][h][:], ACT.Sigmoid, scale=-1.0)
+        nc.scalar.activation(x[1][:], scores[1][0][:], ACT.Relu, bias=neg_cap[:])
+
+        excess = sb.tile([P, TILES, G], F32, name="excess")
+        hit = sb.tile([P, TILES * J], F32, name="hit")
+        prod = hit[:, J - G : J + G].rearrange("p (t g) -> p t g", t=TILES)
+        excess_sum = sb.tile([P, TILES], F32, name="excess_sum")
+        y = sb.tile([P, TILES, G, HALF], F32, name="y")
+        d = sb.tile([P, TILES, G, HALF], F32, name="d")
+        c = [sb.tile([P, G, HALF], F32, name="c%d" % t) for t in range(TILES)]
+
+        def clamp_first(t):
+            nc.vector.tensor_scalar(c[t][:], miss[t][:, 0], floor[:], None, ALU.max)
+
+        def clamp_second(t):
+            nc.vector.scalar_tensor_tensor(d[:, t], miss[t][:, 1], floor[:], c[t][:], ALU.max, ALU.mult)
+
+        def excess_second(t):
+            nc.vector.scalar_tensor_tensor(
+                y[:, t], scores[t][1][:], CAP, x[t][:], ALU.max, ALU.add, accum_out=excess_sum[:, t : t + 1]
+            )
+
+        nc.vector.tensor_scalar(x[0][:], scores[0][0][:], CAP, -CAP, ALU.max, ALU.add)
+        clamp_first(0)
+        excess_second(0)
+        clamp_second(0)
+        clamp_first(1)
+        excess_second(1)
+        clamp_second(1)
+        nc.vector.tensor_reduce(prod, d[:], AX.X, ALU.mult)
+        base = sb.tile([P, TILES], F32, name="base")
+        nc.vector.scalar_tensor_tensor(base[:], excess_sum[:], 1.0 / 64.0, reserve64[:], ALU.mult, ALU.add)
+        nc.vector.tensor_reduce(excess[:], y[:], AX.X, ALU.add)
+
+        logs = [sb.tile([P, G], F32, name="logs%d" % t) for t in range(TILES)]
+        log_sum = sb.tile([P, TILES], F32, name="log_sum")
+        joint = sb.tile([P, G + TILES], F32, name="joint")
+        for t in range(TILES):
+            nc.scalar.activation(
+                logs[t][:], prod[:, t], ACT.Ln, scale=math.exp(HALF * CAP), accum_out=log_sum[:, t : t + 1]
+            )
+        for t in range(TILES):
+            nc.scalar.activation(
+                joint[:, G + t : G + t + 1],
+                log_sum[:, t : t + 1],
+                ACT.Identity,
+                bias=base[:, t : t + 1],
+                scale=-1.0 / 64.0,
+            )
+        hit3 = [hit[:, t * J : (t + 1) * J].rearrange("p (g k) -> p g k", k=GROUP) for t in range(TILES)]
+        for t in range(TILES):
+            nc.scalar.activation(
+                hit3[t].rearrange("p g (h k) -> p g h k", h=2),
+                miss[t][:].rearrange("p h g k -> p g h k"),
+                ACT.Copy,
+                bias=1.0,
+                scale=-1.0,
+            )
+
+        den = sb.tile([P, TILES, G], F32, name="den")
+        for t in range(TILES):
+            nc.vector.scalar_tensor_tensor(
+                den[:, 1 - t], excess[:, t], joint[:, G + t : G + t + 1], logs[t][:], ALU.add, ALU.subtract
+            )
+        nc.vector.tensor_tensor(joint[:, :G], den[:, 0], den[:, 1], ALU.mult)
+        cross = sb.tile([P, TILES, G], F32, name="cross")
+        inv = sb.tile([P, G + TILES], F32, name="inv")
+        nc.vector.tensor_tensor(cross[:], stake8[:], den[:], ALU.mult)
+        nc.vector.reciprocal(inv[:], joint[:])
+
+        e8 = [sb.tile([P, G, 1], F32, name="e8_%d" % t) for t in range(TILES)]
+        e8_sum = sb.tile([P, TILES], F32, name="e8_sum")
+        lead = sb.tile([P, TILES], F32, name="lead")
+        w = sb.tile([P, TILES], F32, name="w")
+
+        def quota(t):
+            nc.vector.scalar_tensor_tensor(
+                e8[t][:, :, 0], cross[:, t], 64.0, inv[:, :G], ALU.mult, ALU.mult, accum_out=e8_sum[:, t : t + 1]
+            )
+
+        quota(0)
+        nc.vector.tensor_tensor(lead[:], inv[:, G:], stake_sum[:], ALU.mult)
+        quota(1)
+        for t in range(TILES):
+            nc.vector.tensor_scalar(
+                w[:, t : t + 1], e8_sum[:, t : t + 1], -1.0 / 64.0, lead[:, t : t + 1], ALU.mult, ALU.add
+            )
+
+        pieces = [(0, 0, G), (1, 0, G // 2), (1, G // 2, G)]
+        grad = [sb.tile([P, hi - lo, GROUP], F32, name="grad%d" % n) for n, (t, lo, hi) in enumerate(pieces)]
+        res = [sb.tile([P, (hi - lo) * GROUP], F32, name="res%d" % n) for n, (t, lo, hi) in enumerate(pieces)]
+
+        def scale_piece(n):
+            t, lo, hi = pieces[n]
+            nc.vector.scalar_tensor_tensor(
+                grad[n][:],
+                e8[t][:, lo:hi].to_broadcast([P, hi - lo, GROUP]),
+                w[:, t : t + 1],
+                hit3[t][:, lo:hi],
+                ALU.subtract,
+                ALU.mult,
+            )
+
+        def finish_piece(n, queue):
+            t, lo, hi = pieces[n]
+            cols_j = slice(lo * GROUP, hi * GROUP)
+            nc.vector.tensor_tensor(res[n][:], grad[n][:].rearrange("p g k -> p (g k)"), old_sb[t][:, cols_j], ALU.add)
+            queue.dma_start(out[t * P : (t + 1) * P, cols_j], res[n][:])
+
+        scale_piece(0)
+        scale_piece(1)
+        finish_piece(0, nc.sync)
+        scale_piece(2)
+        finish_piece(1, nc.scalar)
+        finish_piece(2, nc.sync)

@@ -33,18 +33,18 @@ def tile_attend_bpairquota_kernel(tc, taba, tabb_words, tabb_scales, reserve, st
 
         list_a = sb.tile([P, I // 16], U16, name="list_a")
         list_b = sb.tile([P, J // 16], U16, name="list_b")
-        b_words_all = sb.tile([P, U], U32, name="b_words_all", align_bytes=64)
-        b_scales_all = sb.tile([P, U], U8, name="b_scales_all", align_bytes=64)
-        planes = [sb.tile([P, T], F32, name="plane%d" % r, align_bytes=64) for r in range(PACK)]
-        reserve_sb = sb.tile([P, TILES], F32, name="reserve_sb")
-        stake_sb = sb.tile([P, TILES, G], F32, name="stake_sb")
-        old_sb = [sb.tile([P, J], F32, name="old%d" % t) for t in range(TILES)]
+        b_words_all = sb.tile([P, U], U32, name="b_words_all", tag="words_then_stake", align_bytes=64)
+        b_scales_all = sb.tile([P, U], U8, name="b_scales_all", tag="scales_then_reserve", align_bytes=64)
+        planes01 = sb.tile([P, 2, T], F32, name="planes01", tag="planes_then_old", align_bytes=64)
+        plane2 = sb.tile([P, T], F32, name="plane2", align_bytes=64)
+        plane3 = sb.tile([P, T], F32, name="plane3", align_bytes=64)
 
         nc.vector.memset(b_scales_all[:].bitcast(I32), 0)
         neg_cap = sb.tile([P, 1], F32, name="neg_cap")
         nc.vector.memset(neg_cap[:], -CAP)
 
         nc.sync.dma_start(list_b[:], offs2)
+        nc.sync.dma_start(list_a[:], offs)
         for q in range(4):
             nc.scalar.dma_start(
                 b_scales_all[32 * q : 32 * q + 4, :].bitcast(I32),
@@ -54,22 +54,17 @@ def tile_attend_bpairquota_kernel(tc, taba, tabb_words, tabb_scales, reserve, st
             b_words_all[:].bitcast(I32),
             tabb_words[0].rearrange("p n r -> p (n r)").bitcast(I32),
         )
-        nc.sync.dma_start(list_a[:], offs)
         taba_planes = taba.rearrange("(p r) t -> p r t", r=PACK)
-        for r in range(PACK):
-            nc.sync.dma_start(planes[r][:], taba_planes[:, r, :])
-        nc.sync.dma_start(stake_sb[:], stake.rearrange("(t p) g -> p t g", p=P))
-        with nc.allow_non_contiguous_dma(reason="one reserve value for each row"):
-            nc.sync.dma_start(reserve_sb[:], reserve.rearrange("(t p) o -> p (t o)", p=P))
-        for t in range(TILES):
-            nc.sync.dma_start(old_sb[t][:], old[t * P : (t + 1) * P, :])
+        nc.sync.dma_start(planes01[:], taba_planes[:, 0:2, :])
+        nc.sync.dma_start(plane2[:], taba_planes[:, 2, :])
+        nc.sync.dma_start(plane3[:], taba_planes[:, 3, :])
 
         floor = sb.tile([P, 1], F32, name="floor")
         nc.scalar.activation(floor[:], neg_cap[:], ACT.Sigmoid)
 
         b_scales = sb.tile([P, J], U8, name="b_scales", align_bytes=64)
         b_words = sb.tile([P, J], U32, name="b_words", align_bytes=64)
-        b_scales_listed = sb.tile([P, J], U8, name="b_scales_listed", align_bytes=64)
+        b_scales_listed = sb.tile([P, J], U8, name="b_scales_listed", tag="listed", align_bytes=64)
         nc.vector.tensor_copy(b_scales_listed[:], b_scales_all[:].indirect(list_b[:]))
         nc.vector.tensor_copy(
             b_words[:].rearrange("p (h g k) -> p g h k", h=2, k=HALF), b_words_all[:].indirect(list_b[:])
@@ -85,14 +80,21 @@ def tile_attend_bpairquota_kernel(tc, taba, tabb_words, tabb_scales, reserve, st
         scores = [[ps.tile([P, G, HALF], F32, name="scores%d_%d" % (t, h)) for h in range(2)] for t in range(TILES)]
         cols = P // 16
 
-        def gather(r, t):
-            nc.vector.tensor_copy(woven[t][:, :, r], planes[r][:].indirect(list_a[:, t * cols : (t + 1) * cols]))
-
-        for r in range(PACK - 1):
-            for t in range(TILES):
-                gather(r, t)
+        listed01 = sb.tile([P, 2, I], F32, name="listed01", tag="listed", align_bytes=64)
+        for r in range(2):
+            nc.vector.tensor_copy(listed01[:, r], planes01[:, r].indirect(list_a[:]))
         for t in range(TILES):
-            gather(PACK - 1, t)
+            nc.scalar.activation(
+                woven[t][:, :, 0:2], listed01[:, :, t * P : (t + 1) * P].rearrange("p r i -> p i r"), ACT.Copy
+            )
+
+        def gather(plane, r, t):
+            nc.vector.tensor_copy(woven[t][:, :, r], plane[:].indirect(list_a[:, t * cols : (t + 1) * cols]))
+
+        for t in range(TILES):
+            gather(plane2, 2, t)
+        for t in range(TILES):
+            gather(plane3, 3, t)
             nc.vector.quantize_mx(
                 out=a_words[t][:].bitcast(FP8X4),
                 scales=a_scales[t][:],
@@ -108,6 +110,14 @@ def tile_attend_bpairquota_kernel(tc, taba, tabb_words, tabb_scales, reserve, st
                     start=True,
                     stop=True,
                 )
+
+        old_sb = sb.tile([P, TILES, J], F32, name="old_sb", tag="planes_then_old", align_bytes=64)
+        stake_sb = sb.tile([P, TILES, G], F32, name="stake_sb", tag="words_then_stake", align_bytes=64)
+        reserve_sb = sb.tile([P, TILES], F32, name="reserve_sb", tag="scales_then_reserve", align_bytes=64)
+        nc.sync.dma_start(stake_sb[:], stake.rearrange("(t p) g -> p t g", p=P))
+        with nc.allow_non_contiguous_dma(reason="one reserve value for each row"):
+            nc.sync.dma_start(reserve_sb[:], reserve.rearrange("(t p) o -> p (t o)", p=P))
+        nc.sync.dma_start(old_sb[:], old.rearrange("(t p) j -> p t j", p=P))
 
         stake_sum = sb.tile([P, TILES], F32, name="stake_sum")
         stake8 = sb.tile([P, TILES, G], F32, name="stake8")
@@ -149,27 +159,23 @@ def tile_attend_bpairquota_kernel(tc, taba, tabb_words, tabb_scales, reserve, st
         excess_second(0)
         clamp_second(0)
         clamp_first(1)
-        excess_second(1)
         clamp_second(1)
         nc.vector.tensor_reduce(prod, d[:], AX.X, ALU.mult)
+        excess_second(1)
         base = sb.tile([P, TILES], F32, name="base")
         nc.vector.scalar_tensor_tensor(base[:], excess_sum[:], 1.0 / 64.0, reserve64[:], ALU.mult, ALU.add)
         nc.vector.tensor_reduce(excess[:], y[:], AX.X, ALU.add)
 
         logs = [sb.tile([P, G], F32, name="logs%d" % t) for t in range(TILES)]
         log_sum = sb.tile([P, TILES], F32, name="log_sum")
-        joint = sb.tile([P, G + TILES], F32, name="joint")
+        total = sb.tile([P, TILES], F32, name="total")
         for t in range(TILES):
             nc.scalar.activation(
                 logs[t][:], prod[:, t], ACT.Ln, scale=math.exp(HALF * CAP), accum_out=log_sum[:, t : t + 1]
             )
         for t in range(TILES):
-            nc.scalar.activation(
-                joint[:, G + t : G + t + 1],
-                log_sum[:, t : t + 1],
-                ACT.Identity,
-                bias=base[:, t : t + 1],
-                scale=-1.0 / 64.0,
+            nc.vector.tensor_scalar(
+                total[:, t : t + 1], log_sum[:, t : t + 1], -1.0 / 64.0, base[:, t : t + 1], ALU.mult, ALU.add
             )
         hit3 = [hit[:, t * J : (t + 1) * J].rearrange("p (g k) -> p g k", k=GROUP) for t in range(TILES)]
         for t in range(TILES):
@@ -181,30 +187,25 @@ def tile_attend_bpairquota_kernel(tc, taba, tabb_words, tabb_scales, reserve, st
                 scale=-1.0,
             )
 
-        den = sb.tile([P, TILES, G], F32, name="den")
-        for t in range(TILES):
-            nc.vector.scalar_tensor_tensor(
-                den[:, 1 - t], excess[:, t], joint[:, G + t : G + t + 1], logs[t][:], ALU.add, ALU.subtract
-            )
-        nc.vector.tensor_tensor(joint[:, :G], den[:, 0], den[:, 1], ALU.mult)
-        cross = sb.tile([P, TILES, G], F32, name="cross")
-        inv = sb.tile([P, G + TILES], F32, name="inv")
-        nc.vector.tensor_tensor(cross[:], stake8[:], den[:], ALU.mult)
-        nc.vector.reciprocal(inv[:], joint[:])
-
+        den = [sb.tile([P, G], F32, name="den%d" % t) for t in range(TILES)]
+        inv = [sb.tile([P, G], F32, name="inv%d" % t) for t in range(TILES)]
         e8 = [sb.tile([P, G, 1], F32, name="e8_%d" % t) for t in range(TILES)]
+        inv_total = sb.tile([P, TILES], F32, name="inv_total")
         e8_sum = sb.tile([P, TILES], F32, name="e8_sum")
         lead = sb.tile([P, TILES], F32, name="lead")
         w = sb.tile([P, TILES], F32, name="w")
-
-        def quota(t):
+        for t in range(TILES):
             nc.vector.scalar_tensor_tensor(
-                e8[t][:, :, 0], cross[:, t], 64.0, inv[:, :G], ALU.mult, ALU.mult, accum_out=e8_sum[:, t : t + 1]
+                den[t][:], excess[:, t], total[:, t : t + 1], logs[t][:], ALU.add, ALU.subtract
             )
-
-        quota(0)
-        nc.vector.tensor_tensor(lead[:], inv[:, G:], stake_sum[:], ALU.mult)
-        quota(1)
+        nc.vector.reciprocal(inv_total[:], total[:])
+        nc.vector.reciprocal(inv[0][:], den[0][:])
+        nc.vector.tensor_tensor(lead[:], inv_total[:], stake_sum[:], ALU.mult)
+        nc.vector.reciprocal(inv[1][:], den[1][:])
+        for t in range(TILES):
+            nc.vector.scalar_tensor_tensor(
+                e8[t][:, :, 0], stake8[:, t], 64.0, inv[t][:], ALU.mult, ALU.mult, accum_out=e8_sum[:, t : t + 1]
+            )
         for t in range(TILES):
             nc.vector.tensor_scalar(
                 w[:, t : t + 1], e8_sum[:, t : t + 1], -1.0 / 64.0, lead[:, t : t + 1], ALU.mult, ALU.add
@@ -228,7 +229,7 @@ def tile_attend_bpairquota_kernel(tc, taba, tabb_words, tabb_scales, reserve, st
         def finish_piece(n, queue):
             t, lo, hi = pieces[n]
             cols_j = slice(lo * GROUP, hi * GROUP)
-            nc.vector.tensor_tensor(res[n][:], grad[n][:].rearrange("p g k -> p (g k)"), old_sb[t][:, cols_j], ALU.add)
+            nc.vector.tensor_tensor(res[n][:], grad[n][:].rearrange("p g k -> p (g k)"), old_sb[:, t, cols_j], ALU.add)
             queue.dma_start(out[t * P : (t + 1) * P, cols_j], res[n][:])
 
         scale_piece(0)

@@ -33,38 +33,37 @@ def tile_attend_bpairquota_kernel(tc, taba, tabb_words, tabb_scales, reserve, st
 
         list_a = sb.tile([P, I // 16], U16, name="list_a")
         list_b = sb.tile([P, J // 16], U16, name="list_b")
-        b_words_all = sb.tile([P, U], U32, name="b_words_all", tag="words_then_stake", align_bytes=64)
         b_scales_all = sb.tile([P, U], U8, name="b_scales_all", tag="scales_then_reserve", align_bytes=64)
-        planes01 = sb.tile([P, 2, T], F32, name="planes01", tag="planes_then_old", align_bytes=64)
-        plane2 = sb.tile([P, T], F32, name="plane2", align_bytes=64)
-        plane3 = sb.tile([P, T], F32, name="plane3", align_bytes=64)
-
+        plane0 = sb.tile([P, T], F32, name="plane0", align_bytes=64)
+        unit = sb.tile([P, 1], F32, name="unit", tag="unit_words_stake", align_bytes=64)
+        neg_cap = sb.tile([P, 1], F32, name="neg_cap", tag="cap_planes_old", align_bytes=64)
         nc.vector.memset(b_scales_all[:].bitcast(I32), 0)
-        neg_cap = sb.tile([P, 1], F32, name="neg_cap")
-        nc.vector.memset(neg_cap[:], -CAP)
+        nc.vector.memset(unit[:], 1.0)
+        nc.vector.tensor_scalar(neg_cap[:], unit[:], -CAP, None, ALU.mult)
+        floor = sb.tile([P, 1], F32, name="floor")
+        nc.scalar.activation(floor[:], neg_cap[:], ACT.Sigmoid)
 
-        nc.sync.dma_start(list_b[:], offs2)
+        taba_planes = taba.rearrange("(p r) t -> p r t", r=PACK)
         nc.sync.dma_start(list_a[:], offs)
+        nc.sync.dma_start(list_b[:], offs2)
+        nc.sync.dma_start(plane0[:], taba_planes[:, 0, :])
         for q in range(4):
-            nc.scalar.dma_start(
+            nc.sync.dma_start(
                 b_scales_all[32 * q : 32 * q + 4, :].bitcast(I32),
                 tabb_scales[0, 4 * q : 4 * q + 4, :].bitcast(I32),
             )
+        b_words_all = sb.tile([P, U], U32, name="b_words_all", tag="unit_words_stake", align_bytes=64)
         nc.sync.dma_start(
             b_words_all[:].bitcast(I32),
             tabb_words[0].rearrange("p n r -> p (n r)").bitcast(I32),
         )
-        taba_planes = taba.rearrange("(p r) t -> p r t", r=PACK)
-        nc.sync.dma_start(planes01[:], taba_planes[:, 0:2, :])
-        nc.sync.dma_start(plane2[:], taba_planes[:, 2, :])
-        nc.sync.dma_start(plane3[:], taba_planes[:, 3, :])
-
-        floor = sb.tile([P, 1], F32, name="floor")
-        nc.scalar.activation(floor[:], neg_cap[:], ACT.Sigmoid)
+        planes = sb.tile([P, PACK - 1, T], F32, name="planes", tag="cap_planes_old", align_bytes=64)
+        for r in range(1, PACK):
+            nc.sync.dma_start(planes[:, r - 1], taba_planes[:, r, :])
 
         b_scales = sb.tile([P, J], U8, name="b_scales", align_bytes=64)
         b_words = sb.tile([P, J], U32, name="b_words", align_bytes=64)
-        b_scales_listed = sb.tile([P, J], U8, name="b_scales_listed", tag="listed", align_bytes=64)
+        b_scales_listed = sb.tile([P, J], U8, name="b_scales_listed", align_bytes=64)
         nc.vector.tensor_copy(b_scales_listed[:], b_scales_all[:].indirect(list_b[:]))
         nc.vector.tensor_copy(
             b_words[:].rearrange("p (h g k) -> p g h k", h=2, k=HALF), b_words_all[:].indirect(list_b[:])
@@ -80,21 +79,21 @@ def tile_attend_bpairquota_kernel(tc, taba, tabb_words, tabb_scales, reserve, st
         scores = [[ps.tile([P, G, HALF], F32, name="scores%d_%d" % (t, h)) for h in range(2)] for t in range(TILES)]
         cols = P // 16
 
-        listed01 = sb.tile([P, 2, I], F32, name="listed01", tag="listed", align_bytes=64)
         for r in range(2):
-            nc.vector.tensor_copy(listed01[:, r], planes01[:, r].indirect(list_a[:]))
-        for t in range(TILES):
-            nc.scalar.activation(
-                woven[t][:, :, 0:2], listed01[:, :, t * P : (t + 1) * P].rearrange("p r i -> p i r"), ACT.Copy
-            )
+            plane_bf = sb.tile([P, T], BF16, name="plane_bf%d" % r, align_bytes=64)
+            nc.scalar.activation(plane_bf[:], plane0[:] if r == 0 else planes[:, 0], ACT.Copy)
+            for t in range(TILES):
+                nc.scalar.activation(
+                    woven[t][:, :, r], plane_bf[:].indirect(list_a[:, t * cols : (t + 1) * cols]), ACT.Copy
+                )
 
-        def gather(plane, r, t):
-            nc.vector.tensor_copy(woven[t][:, :, r], plane[:].indirect(list_a[:, t * cols : (t + 1) * cols]))
+        def gather(r, t):
+            nc.vector.tensor_copy(woven[t][:, :, r], planes[:, r - 1].indirect(list_a[:, t * cols : (t + 1) * cols]))
 
         for t in range(TILES):
-            gather(plane2, 2, t)
+            gather(2, t)
         for t in range(TILES):
-            gather(plane3, 3, t)
+            gather(3, t)
             nc.vector.quantize_mx(
                 out=a_words[t][:].bitcast(FP8X4),
                 scales=a_scales[t][:],
@@ -111,8 +110,8 @@ def tile_attend_bpairquota_kernel(tc, taba, tabb_words, tabb_scales, reserve, st
                     stop=True,
                 )
 
-        old_sb = sb.tile([P, TILES, J], F32, name="old_sb", tag="planes_then_old", align_bytes=64)
-        stake_sb = sb.tile([P, TILES, G], F32, name="stake_sb", tag="words_then_stake", align_bytes=64)
+        old_sb = sb.tile([P, TILES, J], F32, name="old_sb", tag="cap_planes_old", align_bytes=64)
+        stake_sb = sb.tile([P, TILES, G], F32, name="stake_sb", tag="unit_words_stake", align_bytes=64)
         reserve_sb = sb.tile([P, TILES], F32, name="reserve_sb", tag="scales_then_reserve", align_bytes=64)
         nc.sync.dma_start(stake_sb[:], stake.rearrange("(t p) g -> p t g", p=P))
         with nc.allow_non_contiguous_dma(reason="one reserve value for each row"):
@@ -133,7 +132,6 @@ def tile_attend_bpairquota_kernel(tc, taba, tabb_words, tabb_scales, reserve, st
         for t in range(TILES):
             for h in range(2):
                 nc.scalar.activation(miss[t][:, h], scores[t][h][:], ACT.Sigmoid, scale=-1.0)
-        nc.scalar.activation(x[1][:], scores[1][0][:], ACT.Relu, bias=neg_cap[:])
 
         excess = sb.tile([P, TILES, G], F32, name="excess")
         hit = sb.tile([P, TILES * J], F32, name="hit")
@@ -154,14 +152,18 @@ def tile_attend_bpairquota_kernel(tc, taba, tabb_words, tabb_scales, reserve, st
                 y[:, t], scores[t][1][:], CAP, x[t][:], ALU.max, ALU.add, accum_out=excess_sum[:, t : t + 1]
             )
 
-        nc.vector.tensor_scalar(x[0][:], scores[0][0][:], CAP, -CAP, ALU.max, ALU.add)
+        def excess_first(t):
+            nc.vector.tensor_scalar(x[t][:], scores[t][0][:], CAP, -CAP, ALU.max, ALU.add)
+
+        excess_first(0)
         clamp_first(0)
         excess_second(0)
         clamp_second(0)
         clamp_first(1)
+        excess_first(1)
         clamp_second(1)
-        nc.vector.tensor_reduce(prod, d[:], AX.X, ALU.mult)
         excess_second(1)
+        nc.vector.tensor_reduce(prod, d[:], AX.X, ALU.mult)
         base = sb.tile([P, TILES], F32, name="base")
         nc.vector.scalar_tensor_tensor(base[:], excess_sum[:], 1.0 / 64.0, reserve64[:], ALU.mult, ALU.add)
         nc.vector.tensor_reduce(excess[:], y[:], AX.X, ALU.add)

import math
from contextlib import ExitStack

import concourse.mybir as mybir

D, T, U, I, J, G = 512, 1024, 1024, 256, 512, 64
FLOPS = 2 * I * J * D

F32 = mybir.dt.float32
BF16 = mybir.dt.bfloat16
I32 = mybir.dt.int32
U32 = mybir.dt.uint32
U16 = mybir.dt.uint16
U8 = mybir.dt.uint8
FP8X4 = mybir.dt.float8_e4m3fn_x4
ALU = mybir.AluOpType
ACT = mybir.ActivationFunctionType
AX = mybir.AxisListType

P = 128
PACK = 4
TILES = I // P
GROUP = J // G
HALF = GROUP // 2
CAP = 10.875


def tile_attend_bpairquota_kernel(tc, taba, tabb_words, tabb_scales, reserve, stake, old, offs, offs2, out):
    nc = tc.nc
    with ExitStack() as ctx:
        sb = ctx.enter_context(tc.tile_pool(name="sb", bufs=1))
        ps = ctx.enter_context(tc.psum_pool(name="ps", bufs=1))

        list_a = sb.tile([P, I // 16], U16, name="list_a")
        list_b = sb.tile([P, J // 16], U16, name="list_b")
        b_scales_all = sb.tile([P, U], U8, name="b_scales_all", tag="scales_then_reserve", align_bytes=64)
        plane0 = sb.tile([P, T], F32, name="plane0", align_bytes=64)
        unit = sb.tile([P, 1], F32, name="unit", tag="unit_words_stake", align_bytes=64)
        neg_cap = sb.tile([P, 1], F32, name="neg_cap", tag="cap_planes_old", align_bytes=64)
        nc.vector.memset(b_scales_all[:].bitcast(I32), 0)
        nc.vector.memset(unit[:], 1.0)
        nc.vector.tensor_scalar(neg_cap[:], unit[:], -CAP, None, ALU.mult)
        floor = sb.tile([P, 1], F32, name="floor")
        nc.scalar.activation(floor[:], neg_cap[:], ACT.Sigmoid)

        taba_planes = taba.rearrange("(p r) t -> p r t", r=PACK)
        nc.sync.dma_start(list_a[:], offs)
        nc.sync.dma_start(list_b[:], offs2)
        nc.sync.dma_start(plane0[:], taba_planes[:, 0, :])
        for q in range(4):
            nc.sync.dma_start(
                b_scales_all[32 * q : 32 * q + 4, :].bitcast(I32),
                tabb_scales[0, 4 * q : 4 * q + 4, :].bitcast(I32),
            )
        b_words_all = sb.tile([P, U], U32, name="b_words_all", tag="unit_words_stake", align_bytes=64)
        nc.sync.dma_start(
            b_words_all[:].bitcast(I32),
            tabb_words[0].rearrange("p n r -> p (n r)").bitcast(I32),
        )
        planes = sb.tile([P, PACK - 1, T], F32, name="planes", tag="cap_planes_old", align_bytes=64)
        for r in range(1, PACK):
            nc.sync.dma_start(planes[:, r - 1], taba_planes[:, r, :])

        b_scales = sb.tile([P, J], U8, name="b_scales", align_bytes=64)
        b_words = sb.tile([P, J], U32, name="b_words", align_bytes=64)
        b_scales_listed = sb.tile([P, J], U8, name="b_scales_listed", align_bytes=64)
        nc.vector.tensor_copy(b_scales_listed[:], b_scales_all[:].indirect(list_b[:]))
        nc.vector.tensor_copy(
            b_words[:].rearrange("p (h g k) -> p g h k", h=2, k=HALF), b_words_all[:].indirect(list_b[:])
        )
        nc.vector.tensor_copy(
            b_scales[:].bitcast(I32).rearrange("p (h g) -> p h g", h=2),
            b_scales_listed[:].bitcast(I32).rearrange("p (g h) -> p h g", h=2),
        )

        woven = [sb.tile([P, P, PACK], BF16, name="woven%d" % t, align_bytes=64) for t in range(TILES)]
        a_words = [sb.tile([P, P], U32, name="a_words%d" % t, align_bytes=64) for t in range(TILES)]
        a_scales = [sb.tile([P, P], U8, name="a_scales%d" % t, align_bytes=64) for t in range(TILES)]
        scores = [[ps.tile([P, G, HALF], F32, name="scores%d_%d" % (t, h)) for h in range(2)] for t in range(TILES)]
        cols = P // 16

        for r in range(2):
            plane_bf = sb.tile([P, T], BF16, name="plane_bf%d" % r, align_bytes=64)
            nc.scalar.activation(plane_bf[:], plane0[:] if r == 0 else planes[:, 0], ACT.Copy)
            for t in range(TILES):
                nc.scalar.activation(
                    woven[t][:, :, r], plane_bf[:].indirect(list_a[:, t * cols : (t + 1) * cols]), ACT.Copy
                )

        def gather(r, t):
            nc.vector.tensor_copy(woven[t][:, :, r], planes[:, r - 1].indirect(list_a[:, t * cols : (t + 1) * cols]))

        for t in range(TILES):
            gather(2, t)
        for t in range(TILES):
            gather(3, t)
            nc.vector.quantize_mx(
                out=a_words[t][:].bitcast(FP8X4),
                scales=a_scales[t][:],
                in_=woven[t][:].rearrange("p i r -> p (i r)"),
            )
            for h in range(2):
                nc.tensor.matmul_mx(
                    out=scores[t][h][:].rearrange("p g k -> p (g k)"),
                    lhsT=a_words[t][:].bitcast(FP8X4),
                    lhsT_scale=a_scales[t][:],
                    rhs=b_words[:, h * (J // 2) : (h + 1) * (J // 2)].bitcast(FP8X4),
                    rhs_scale=b_scales[:, h * (J // 2) : (h + 1) * (J // 2)],
                    start=True,
                    stop=True,
                )

        old_sb = sb.tile([P, TILES, J], F32, name="old_sb", tag="cap_planes_old", align_bytes=64)
        stake_sb = sb.tile([P, TILES, G], F32, name="stake_sb", tag="unit_words_stake", align_bytes=64)
        reserve_sb = sb.tile([P, TILES], F32, name="reserve_sb", tag="scales_then_reserve", align_bytes=64)
        nc.sync.dma_start(stake_sb[:], stake.rearrange("(t p) g -> p t g", p=P))
        with nc.allow_non_contiguous_dma(reason="one reserve value for each row"):
            nc.sync.dma_start(reserve_sb[:], reserve.rearrange("(t p) o -> p (t o)", p=P))
        nc.sync.dma_start(old_sb[:], old.rearrange("(t p) j -> p t j", p=P))

        stake_sum = sb.tile([P, TILES], F32, name="stake_sum")
        stake8 = sb.tile([P, TILES, G], F32, name="stake8")
        for t in range(TILES):
            nc.scalar.activation(
                stake8[:, t], stake_sb[:, t], ACT.Copy, scale=1.0 / 8.0, accum_out=stake_sum[:, t : t + 1]
            )
        reserve64 = sb.tile([P, TILES], F32, name="reserve64")
        nc.scalar.activation(reserve64[:], reserve_sb[:], ACT.Copy, scale=1.0 / 64.0)

        miss = [sb.tile([P, 2, G, HALF], F32, name="miss%d" % t) for t in range(TILES)]
        x = [sb.tile([P, G, HALF], F32, name="x%d" % t) for t in range(TILES)]
        for t in range(TILES):
            for h in range(2):
                nc.scalar.activation(miss[t][:, h], scores[t][h][:], ACT.Sigmoid, scale=-1.0)

        excess = sb.tile([P, TILES, G], F32, name="excess")
        hit = sb.tile([P, TILES * J], F32, name="hit")
        prod = hit[:, J - G : J + G].rearrange("p (t g) -> p t g", t=TILES)
        excess_sum = sb.tile([P, TILES], F32, name="excess_sum")
        y = sb.tile([P, TILES, G, HALF], F32, name="y")
        d = sb.tile([P, TILES, G, HALF], F32, name="d")
        c = [sb.tile([P, G, HALF], F32, name="c%d" % t) for t in range(TILES)]

        def clamp_first(t):
            nc.vector.tensor_scalar(c[t][:], miss[t][:, 0], floor[:], None, ALU.max)

        def clamp_second(t):
            nc.vector.scalar_tensor_tensor(d[:, t], miss[t][:, 1], floor[:], c[t][:], ALU.max, ALU.mult)

        def excess_second(t):
            nc.vector.scalar_tensor_tensor(
                y[:, t], scores[t][1][:], CAP, x[t][:], ALU.max, ALU.add, accum_out=excess_sum[:, t : t + 1]
            )

        def excess_first(t):
            nc.vector.tensor_scalar(x[t][:], scores[t][0][:], CAP, -CAP, ALU.max, ALU.add)

        excess_first(0)
        clamp_first(0)
        excess_second(0)
        clamp_second(0)
        clamp_first(1)
        excess_first(1)
        clamp_second(1)
        excess_second(1)
        nc.vector.tensor_reduce(prod, d[:], AX.X, ALU.mult)
        base = sb.tile([P, TILES], F32, name="base")
        nc.vector.scalar_tensor_tensor(base[:], excess_sum[:], 1.0 / 64.0, reserve64[:], ALU.mult, ALU.add)
        nc.vector.tensor_reduce(excess[:], y[:], AX.X, ALU.add)

        logs = [sb.tile([P, G], F32, name="logs%d" % t) for t in range(TILES)]
        log_sum = sb.tile([P, TILES], F32, name="log_sum")
        total = sb.tile([P, TILES], F32, name="total")
        for t in range(TILES):
            nc.scalar.activation(
                logs[t][:], prod[:, t], ACT.Ln, scale=math.exp(HALF * CAP), accum_out=log_sum[:, t : t + 1]
            )
        for t in range(TILES):
            nc.vector.tensor_scalar(
                total[:, t : t + 1], log_sum[:, t : t + 1], -1.0 / 64.0, base[:, t : t + 1], ALU.mult, ALU.add
            )
        hit3 = [hit[:, t * J : (t + 1) * J].rearrange("p (g k) -> p g k", k=GROUP) for t in range(TILES)]
        for t in range(TILES):
            nc.scalar.activation(
                hit3[t].rearrange("p g (h k) -> p g h k", h=2),
                miss[t][:].rearrange("p h g k -> p g h k"),
                ACT.Copy,
                bias=1.0,
                scale=-1.0,
            )

        den = [sb.tile([P, G], F32, name="den%d" % t) for t in range(TILES)]
        inv = [sb.tile([P, G], F32, name="inv%d" % t) for t in range(TILES)]
        e8 = [sb.tile([P, G, 1], F32, name="e8_%d" % t) for t in range(TILES)]
        inv_total = sb.tile([P, TILES], F32, name="inv_total")
        e8_sum = sb.tile([P, TILES], F32, name="e8_sum")
        lead = sb.tile([P, TILES], F32, name="lead")
        w = sb.tile([P, TILES], F32, name="w")
        for t in range(TILES):
            nc.vector.scalar_tensor_tensor(
                den[t][:], excess[:, t], total[:, t : t + 1], logs[t][:], ALU.add, ALU.subtract
            )
        nc.vector.reciprocal(inv_total[:], total[:])
        nc.vector.reciprocal(inv[0][:], den[0][:])
        nc.vector.tensor_tensor(lead[:], inv_total[:], stake_sum[:], ALU.mult)
        nc.vector.reciprocal(inv[1][:], den[1][:])
        for t in range(TILES):
            nc.vector.scalar_tensor_tensor(
                e8[t][:, :, 0], stake8[:, t], 64.0, inv[t][:], ALU.mult, ALU.mult, accum_out=e8_sum[:, t : t + 1]
            )
        for t in range(TILES):
            nc.vector.tensor_scalar(
                w[:, t : t + 1], e8_sum[:, t : t + 1], -1.0 / 64.0, lead[:, t : t + 1], ALU.mult, ALU.add
            )

        pieces = [(0, 0, G), (1, 0, G // 2), (1, G // 2, G)]
        grad = [sb.tile([P, hi - lo, GROUP], F32, name="grad%d" % n) for n, (t, lo, hi) in enumerate(pieces)]
        res = [sb.tile([P, (hi - lo) * GROUP], F32, name="res%d" % n) for n, (t, lo, hi) in enumerate(pieces)]

        def scale_piece(n):
            t, lo, hi = pieces[n]
            nc.vector.scalar_tensor_tensor(
                grad[n][:],
                e8[t][:, lo:hi].to_broadcast([P, hi - lo, GROUP]),
                w[:, t : t + 1],
                hit3[t][:, lo:hi],
                ALU.subtract,
                ALU.mult,
            )

        def finish_piece(n, queue):
            t, lo, hi = pieces[n]
            cols_j = slice(lo * GROUP, hi * GROUP)
            nc.vector.tensor_tensor(res[n][:], grad[n][:].rearrange("p g k -> p (g k)"), old_sb[:, t, cols_j], ALU.add)
            queue.dma_start(out[t * P : (t + 1) * P, cols_j], res[n][:])

        scale_piece(0)
        scale_piece(1)
        finish_piece(0, nc.sync)
        scale_piece(2)
        finish_piece(1, nc.scalar)
        finish_piece(2, nc.sync)
